import numpy as np
import ml_dtypes


def mxq(x, axis, fmt="e4m3"):
    dtype, down = {"e4m3": (ml_dtypes.float8_e4m3fn, 7), "e5m2": (ml_dtypes.float8_e5m2, 14)}[fmt]
    v = np.moveaxis(np.asarray(x, np.float32).astype(ml_dtypes.bfloat16).astype(np.float64), axis, -1)
    blocks = v.reshape(v.shape[:-1] + (-1, 32))
    amax = np.abs(blocks).max(-1, keepdims=True)
    byte = np.maximum(np.where(amax > 0, np.frexp(amax)[1] - 1 + 127, 0) - down, 1)
    scale = np.exp2(byte - 127.0)
    codes = (blocks / scale).astype(np.float32).astype(dtype).astype(np.float64)
    return np.moveaxis((codes * scale).reshape(v.shape), -1, axis)


WIDE = False


def mx_kscale(k):
    if not WIDE:
        return np.ones(k)
    levels = np.array([10, -10, 5, -5, 0])
    if k % 512:
        return np.exp2(np.random.permutation(np.resize(levels, k // 32))).repeat(32)
    a = np.empty((k // 512, 16))
    for p in range(k // 512):
        a[p, :8] = np.random.permutation(np.resize(levels, 8))
        for g in range(8):
            far = levels[np.abs(levels - a[p, g]) >= 10]
            a[p, g + 8] = far[np.random.randint(len(far))]
    return np.exp2(a.ravel()).repeat(32)


def f64(x):
    return np.asarray(x).astype(np.float64)


def striped(idx):
    return np.tile(idx.reshape(-1, 16).T, (8, 1)).astype(np.uint16)


def unstriped(offs):
    return offs[:16].T.reshape(-1).astype(np.int64)


K, T, E, C, N = 512, 2048, 16, 128, 256


def by_expert(wq, xq):
    return np.concatenate([wq[e].T @ xq[:, e * C:(e + 1) * C] for e in range(E)], axis=1)


def setup_inputs():
    n = np.random.standard_normal
    s = mx_kscale(K)[:, None]
    return {
        "xT": (n((K, T)) * s).astype(np.float32),
        "w": (n((E, K, N)) / np.sqrt(K) / s[None]).astype(np.float32),
        "offs": striped(np.random.permutation(T)[:E * C]),
    }


def reference(xT, w, offs):
    idx = unstriped(offs)
    xq = mxq(f64(xT)[:, idx], 0, "e4m3")
    y = by_expert(mxq(f64(w), 1, "e4m3"), xq)
    out = np.zeros((N, T))
    out[:, idx] = y
    return out

@@ -1,0 +1,165 @@
+from contextlib import ExitStack
+
+import concourse.mybir as mybir
+
+K, T, E, C, N = 512, 2048, 16, 128, 256
+FLOPS = 2 * K * N * E * C
+
+F32 = mybir.dt.float32
+BF16 = mybir.dt.bfloat16
+U32 = mybir.dt.uint32
+U16 = mybir.dt.uint16
+U8 = mybir.dt.uint8
+FP8X4 = mybir.dt.float8_e4m3fn_x4
+MULT = mybir.AluOpType.mult
+ADD = mybir.AluOpType.add
+
+P = 128
+HALF = T // 2
+GRP = 4
+GATHERS = ((0, 512), (512, 512), (1024, 512), (1536, 512))
+CHUNKS = ((0, 256), (256, 256), (512, 512), (1024, 512), (1536, 512))
+CAST_SPLIT = ((("v", 0, 512), ("s", 512, 768), ("g", 768, 1024)), (("s", 0, 512), ("g", 512, 1024)))
+IENG = "gggg"
+DENG = "ssssssss"
+WG_BUFS = 3
+
+
+def tile_routed_moe_kernel(tc, xT, w, offs, out):
+    nc = tc.nc
+    with ExitStack() as ctx:
+        held = ctx.enter_context(tc.tile_pool(name="held", bufs=1))
+        wraw_pool = ctx.enter_context(tc.tile_pool(name="wraw", bufs=6))
+        wgrp_pool = ctx.enter_context(tc.tile_pool(name="wgrp", bufs=WG_BUFS))
+        y_pool = ctx.enter_context(tc.tile_pool(name="ypool", bufs=4))
+        psum = ctx.enter_context(tc.psum_pool(name="psum", bufs=1))
+
+        offsets = held.tile([P, E * C // 16], U16, name="offsets")
+        nc.sync.dma_start(offsets[:], offs)
+
+        x_view = xT.rearrange("(p t) n -> p t n", t=4)
+        xraw = {}
+        for u in range(2):
+            for h in range(2):
+                xr = held.tile([P, 2, HALF], F32, name="xraw%d%d" % (u, h))
+                nc.sync.dma_start(xr[:], x_view[:, 2 * u : 2 * u + 2, h * HALF : (h + 1) * HALF])
+                xraw[(u, h)] = xr
+        wraw = []
+        for i in range(E // 2):
+            wr = wraw_pool.tile([P, 2, 4, N], F32, name="wr")
+            nc.sync.dma_start(wr[:], w[2 * i : 2 * i + 2].rearrange("e (p j) n -> p e j n", j=4))
+            wraw.append(wr)
+
+        def copy_on(kind, dst, src):
+            if kind == "v":
+                nc.vector.tensor_copy(dst, src)
+            elif kind == "s":
+                nc.scalar.copy(dst, src)
+            else:
+                nc.gpsimd.tensor_scalar(dst, src, 1.0, 0.0, op0=MULT, op1=ADD)
+
+        xpair = [held.tile([P, 2 * T], BF16, name="xpair%d" % u) for u in range(2)]
+        for u in range(2):
+            for h in range(2):
+                for kind, n0, n1 in CAST_SPLIT[u]:
+                    dst = xpair[u][:, 2 * (h * HALF + n0) : 2 * (h * HALF + n1)]
+                    src = xraw[(u, h)][:, :, n0:n1]
+                    if kind == "g":
+                        copy_on(kind, dst.rearrange("p (n e) -> p n e", e=2), src.rearrange("p e n -> p n e"))
+                    else:
+                        copy_on(
+                            kind,
+                            dst.rearrange("p (c i e) -> p c e i", i=4, e=2),
+                            src.rearrange("p e (c i) -> p c e i", i=4),
+                        )
+
+        NCH = len(CHUNKS)
+        xg = [held.tile([P, 4 * n], BF16, name="xg%d" % i, align_bytes=64) for i, (s0, n) in enumerate(GATHERS)]
+        xw = [held.tile([P, 4 * n], BF16, name="xw%d" % i, align_bytes=64) for i, (s0, n) in enumerate(GATHERS)]
+        xc = [held.tile([P, n], U32, name="xc%d" % i, align_bytes=64) for i, (s0, n) in enumerate(GATHERS)]
+        xs = [held.tile([P, n], U8, name="xs%d" % i, align_bytes=64) for i, (s0, n) in enumerate(GATHERS)]
+        wc = [held.tile([P, n // C * N], U32, name="wc%d" % c, align_bytes=64) for c, (s0, n) in enumerate(CHUNKS)]
+        ws = [held.tile([P, n // C * N], U8, name="ws%d" % c, align_bytes=64) for c, (s0, n) in enumerate(CHUNKS)]
+        acc = [[psum.tile([P, GRP * C], F32, name="acc%d%d" % (mb, g)) for g in range(E // GRP)] for mb in range(2)]
+        win = [held.tile([P, T], F32, name="win%d" % mb) for mb in range(2)]
+        wgs = {}
+        ys = {}
+
+        def offs_of(s0, n):
+            return offsets[:, s0 // 16 : (s0 + n) // 16]
+
+        def gather(u, i):
+            s0, n = GATHERS[i]
+            dst = xw[i][:].bitcast(U32)[:, u * n : (u + 1) * n]
+            nc.vector.tensor_copy(dst, xpair[u][:].bitcast(U32).indirect(offs_of(s0, n)))
+
+        def quant_x(i):
+            copy_on(
+                IENG[i],
+                xg[i][:].rearrange("p (n u e) -> p n u e", u=2, e=2),
+                xw[i][:].rearrange("p (u n e) -> p n u e", u=2, e=2),
+            )
+            nc.vector.quantize_mx(out=xc[i][:].bitcast(FP8X4), scales=xs[i][:], in_=xg[i][:])
+
+        def piece_of(slot):
+            for i, (s0, n) in enumerate(GATHERS):
+                if s0 <= slot < s0 + n:
+                    return i, slot - s0
+            raise ValueError("slot")
+
+        def group_w(c):
+            s0, n = CHUNKS[c]
+            e0, ne = s0 // C, n // C
+            wg = wgrp_pool.tile([P, ne * 4 * N], BF16, name="wg", align_bytes=64)
+            wgs[c] = wg
+            for i in range(e0 // 2, (e0 + ne) // 2):
+                copy_on(
+                    DENG[i],
+                    wg[:, (2 * i - e0) * 4 * N : (2 * i - e0 + 2) * 4 * N].rearrange("p (e c i j) -> p e c j i", e=2, i=4, j=4),
+                    wraw[i][:].rearrange("p e j (c i) -> p e c j i", i=4),
+                )
+
+        def stage_b(c):
+            s0, n = CHUNKS[c]
+            e0, ne = s0 // C, n // C
+            g, q0 = e0 // GRP, e0 % GRP
+            nc.vector.quantize_mx(out=wc[c][:].bitcast(FP8X4), scales=ws[c][:], in_=wgs[c][:])
+            for mb in range(2):
+                for q in range(ne):
+                    wcols = slice(q * N + mb * P, q * N + (mb + 1) * P)
+                    i, r0 = piece_of(s0 + q * C)
+                    nc.tensor.matmul_mx(
+                        out=acc[mb][g][:, (q0 + q) * C : (q0 + q + 1) * C],
+                        lhsT=wc[c][:, wcols].bitcast(FP8X4),
+                        lhsT_scale=ws[c][:, wcols],
+                        rhs=xc[i][:, r0 : r0 + C].bitcast(FP8X4),
+                        rhs_scale=xs[i][:, r0 : r0 + C],
+                        start=True,
+                        stop=True,
+                    )
+                y = y_pool.tile([P, n], F32, name="y")
+                nc.scalar.copy(y[:], acc[mb][g][:, q0 * C : (q0 + ne) * C])
+                ys[(c, mb)] = y
+
+        def scatter(c, mb):
+            s0, n = CHUNKS[c]
+            nc.vector.tensor_copy(win[mb][:].indirect(offs_of(s0, n)), ys[(c, mb)][:])
+
+        for u in range(2):
+            for i in range(len(GATHERS)):
+                gather(u, i)
+        for i in range(len(GATHERS)):
+            quant_x(i)
+        for c in range(min(WG_BUFS, NCH)):
+            group_w(c)
+        stage_b(0)
+        for c in range(1, NCH):
+            if c - 1 + WG_BUFS < NCH:
+                group_w(c - 1 + WG_BUFS)
+            scatter(c - 1, 0)
+            stage_b(c)
+            scatter(c - 1, 1)
+        scatter(NCH - 1, 0)
+        nc.sync.dma_start(out[0:P, :], win[0][:])
+        scatter(NCH - 1, 1)
+        nc.sync.dma_start(out[P : 2 * P, :], win[1][:])

@@ -13,6 +13,7 @@ U8 = mybir.dt.uint8
 FP8X4 = mybir.dt.float8_e4m3fn_x4
 MULT = mybir.AluOpType.mult
 ADD = mybir.AluOpType.add
+COPY = mybir.ActivationFunctionType.Copy
 
 P = 128
 HALF = T // 2
@@ -21,8 +22,9 @@ GATHERS = ((0, 512), (512, 512), (1024, 512), (1536, 512))
 CHUNKS = ((0, 256), (256, 256), (512, 512), (1024, 512), (1536, 512))
 CAST_SPLIT = ((("v", 0, 512), ("s", 512, 768), ("g", 768, 1024)), (("s", 0, 512), ("g", 512, 1024)))
 IENG = "gggg"
-DENG = "ssssssss"
+DENG = "sssssssg"
 WG_BUFS = 3
+SLATE = 3
 
 
 def tile_routed_moe_kernel(tc, xT, w, offs, out):
@@ -32,6 +34,7 @@ def tile_routed_moe_kernel(tc, xT, w, offs, out):
         wraw_pool = ctx.enter_context(tc.tile_pool(name="wraw", bufs=6))
         wgrp_pool = ctx.enter_context(tc.tile_pool(name="wgrp", bufs=WG_BUFS))
         y_pool = ctx.enter_context(tc.tile_pool(name="ypool", bufs=4))
+        reuse = ctx.enter_context(tc.tile_pool(name="reuse", bufs=1))
         psum = ctx.enter_context(tc.psum_pool(name="psum", bufs=1))
 
         offsets = held.tile([P, E * C // 16], U16, name="offsets")
@@ -75,7 +78,7 @@ def tile_routed_moe_kernel(tc, xT, w, offs, out):
 
         NCH = len(CHUNKS)
         xg = [held.tile([P, 4 * n], BF16, name="xg%d" % i, align_bytes=64) for i, (s0, n) in enumerate(GATHERS)]
-        xw = [held.tile([P, 4 * n], BF16, name="xw%d" % i, align_bytes=64) for i, (s0, n) in enumerate(GATHERS)]
+        xw = [(reuse if i >= SLATE - 1 else held).tile([P, 4 * n], BF16, name="xw%d" % i, align_bytes=64) for i, (s0, n) in enumerate(GATHERS)]
         xc = [held.tile([P, n], U32, name="xc%d" % i, align_bytes=64) for i, (s0, n) in enumerate(GATHERS)]
         xs = [held.tile([P, n], U8, name="xs%d" % i, align_bytes=64) for i, (s0, n) in enumerate(GATHERS)]
         wc = [held.tile([P, n // C * N], U32, name="wc%d" % c, align_bytes=64) for c, (s0, n) in enumerate(CHUNKS)]
@@ -93,12 +96,19 @@ def tile_routed_moe_kernel(tc, xT, w, offs, out):
             dst = xw[i][:].bitcast(U32)[:, u * n : (u + 1) * n]
             nc.vector.tensor_copy(dst, xpair[u][:].bitcast(U32).indirect(offs_of(s0, n)))
 
-        def quant_x(i):
-            copy_on(
-                IENG[i],
-                xg[i][:].rearrange("p (n u e) -> p n u e", u=2, e=2),
-                xw[i][:].rearrange("p (u n e) -> p n u e", u=2, e=2),
+        def gather_planes(i, xplane):
+            s0, n = GATHERS[i]
+            for e in range(2):
+                dst = xw[i][:].rearrange("p (u n e) -> p u n e", u=2, e=2)[:, 1, :, e]
+                nc.scalar.activation(dst, xplane[:, e, :].indirect(offs_of(s0, n)), COPY)
+
+        def weave_x(i):
+            nc.gpsimd.tensor_copy(
+                xg[i][:].bitcast(U32).rearrange("p (n u) -> p n u", u=2),
+                xw[i][:].bitcast(U32).rearrange("p (u n) -> p n u", u=2),
             )
+
+        def quant_x(i):
             nc.vector.quantize_mx(out=xc[i][:].bitcast(FP8X4), scales=xs[i][:], in_=xg[i][:])
 
         def piece_of(slot):
@@ -113,11 +123,15 @@ def tile_routed_moe_kernel(tc, xT, w, offs, out):
             wg = wgrp_pool.tile([P, ne * 4 * N], BF16, name="wg", align_bytes=64)
             wgs[c] = wg
             for i in range(e0 // 2, (e0 + ne) // 2):
-                copy_on(
-                    DENG[i],
-                    wg[:, (2 * i - e0) * 4 * N : (2 * i - e0 + 2) * 4 * N].rearrange("p (e c i j) -> p e c j i", e=2, i=4, j=4),
-                    wraw[i][:].rearrange("p e j (c i) -> p e c j i", i=4),
-                )
+                dst = wg[:, (2 * i - e0) * 4 * N : (2 * i - e0 + 2) * 4 * N]
+                if DENG[i] == "g":
+                    copy_on("g", dst.rearrange("p (e n j) -> p e n j", e=2, j=4), wraw[i][:].rearrange("p e j n -> p e n j"))
+                else:
+                    copy_on(
+                        DENG[i],
+                        dst.rearrange("p (e c i j) -> p e c j i", e=2, i=4, j=4),
+                        wraw[i][:].rearrange("p e j (c i) -> p e c j i", i=4),
+                    )
 
         def stage_b(c):
             s0, n = CHUNKS[c]
@@ -137,7 +151,10 @@ def tile_routed_moe_kernel(tc, xT, w, offs, out):
                         start=True,
                         stop=True,
                     )
-                y = y_pool.tile([P, n], F32, name="y")
+                if c == SLATE and mb == 1:
+                    y = reuse.tile([P, n], F32, name="xw%d" % SLATE, align_bytes=64)
+                else:
+                    y = y_pool.tile([P, n], F32, name="y")
                 nc.scalar.copy(y[:], acc[mb][g][:, q0 * C : (q0 + ne) * C])
                 ys[(c, mb)] = y
 
@@ -147,9 +164,14 @@ def tile_routed_moe_kernel(tc, xT, w, offs, out):
 
         for u in range(2):
             for i in range(len(GATHERS)):
-                gather(u, i)
-        for i in range(len(GATHERS)):
+                if u == 0 or i != SLATE:
+                    gather(u, i)
+        for i in range(SLATE):
+            weave_x(i)
             quant_x(i)
+        xplane = reuse.tile([P, 2, T], BF16, name="xw%d" % (SLATE - 1), align_bytes=64)
+        for h in range(2):
+            copy_on("g", xplane[:, :, h * HALF : (h + 1) * HALF], xraw[(1, h)][:])
         for c in range(min(WG_BUFS, NCH)):
             group_w(c)
         stage_b(0)
@@ -157,6 +179,11 @@ def tile_routed_moe_kernel(tc, xT, w, offs, out):
             if c - 1 + WG_BUFS < NCH:
                 group_w(c - 1 + WG_BUFS)
             scatter(c - 1, 0)
+            if c == SLATE:
+                gather_planes(SLATE, xplane)
+                weave_x(SLATE)
+            if c == SLATE + 1:
+                quant_x(SLATE)
             stage_b(c)
             scatter(c - 1, 1)
         scatter(NCH - 1, 0)

@@ -23,7 +23,7 @@ CHUNKS = ((0, 256), (256, 256), (512, 512), (1024, 512), (1536, 512))
 CAST_SPLIT = ((("v", 0, 512), ("s", 512, 768), ("g", 768, 1024)), (("s", 0, 512), ("g", 512, 1024)))
 IENG = "gggg"
 DENG = "sssssssg"
-WG_BUFS = 3
+WG_BUFS = 2
 SLATE = 3
 
 
@@ -79,7 +79,7 @@ def tile_routed_moe_kernel(tc, xT, w, offs, out):
         NCH = len(CHUNKS)
         xg = [held.tile([P, 4 * n], BF16, name="xg%d" % i, align_bytes=64) for i, (s0, n) in enumerate(GATHERS)]
         xw = [(reuse if i >= SLATE - 1 else held).tile([P, 4 * n], BF16, name="xw%d" % i, align_bytes=64) for i, (s0, n) in enumerate(GATHERS)]
-        xc = [held.tile([P, n], U32, name="xc%d" % i, align_bytes=64) for i, (s0, n) in enumerate(GATHERS)]
+        xc = {i: held.tile([P, GATHERS[i][1]], U32, name="xc%d" % i, align_bytes=64) for i in (0, 3)}
         xs = [held.tile([P, n], U8, name="xs%d" % i, align_bytes=64) for i, (s0, n) in enumerate(GATHERS)]
         wc = [held.tile([P, n // C * N], U32, name="wc%d" % c, align_bytes=64) for c, (s0, n) in enumerate(CHUNKS)]
         ws = [held.tile([P, n // C * N], U8, name="ws%d" % c, align_bytes=64) for c, (s0, n) in enumerate(CHUNKS)]
@@ -120,7 +120,10 @@ def tile_routed_moe_kernel(tc, xT, w, offs, out):
         def group_w(c):
             s0, n = CHUNKS[c]
             e0, ne = s0 // C, n // C
-            wg = wgrp_pool.tile([P, ne * 4 * N], BF16, name="wg", align_bytes=64)
+            if c == 2:
+                wg = reuse.tile([P, ne * 4 * N], BF16, name="wg2", align_bytes=64)
+            else:
+                wg = wgrp_pool.tile([P, ne * 4 * N], BF16, name="wg", align_bytes=64)
             wgs[c] = wg
             for i in range(e0 // 2, (e0 + ne) // 2):
                 dst = wg[:, (2 * i - e0) * 4 * N : (2 * i - e0 + 2) * 4 * N]
@@ -153,6 +156,8 @@ def tile_routed_moe_kernel(tc, xT, w, offs, out):
                     )
                 if c == SLATE and mb == 1:
                     y = reuse.tile([P, n], F32, name="xw%d" % SLATE, align_bytes=64)
+                elif c == 0 and mb == 0:
+                    y = reuse.tile([P, n], F32, name="y00", align_bytes=64)
                 else:
                     y = y_pool.tile([P, n], F32, name="y")
                 nc.scalar.copy(y[:], acc[mb][g][:, q0 * C : (q0 + ne) * C])
@@ -166,26 +171,38 @@ def tile_routed_moe_kernel(tc, xT, w, offs, out):
             for i in range(len(GATHERS)):
                 if u == 0 or i != SLATE:
                     gather(u, i)
-        for i in range(SLATE):
-            weave_x(i)
-            quant_x(i)
+        weave_x(0)
+        quant_x(0)
+        weave_x(1)
+        weave_x(2)
         xplane = reuse.tile([P, 2, T], BF16, name="xw%d" % (SLATE - 1), align_bytes=64)
-        for h in range(2):
-            copy_on("g", xplane[:, :, h * HALF : (h + 1) * HALF], xraw[(1, h)][:])
-        for c in range(min(WG_BUFS, NCH)):
-            group_w(c)
+        copy_on("g", xplane[:, :, 0:HALF], xraw[(1, 0)][:])
+        copy_on("g", xplane[:, :, HALF:T], xraw[(1, 1)][:])
+        group_w(0)
+        group_w(1)
+        group_w(2)
         stage_b(0)
-        for c in range(1, NCH):
-            if c - 1 + WG_BUFS < NCH:
-                group_w(c - 1 + WG_BUFS)
-            scatter(c - 1, 0)
-            if c == SLATE:
-                gather_planes(SLATE, xplane)
-                weave_x(SLATE)
-            if c == SLATE + 1:
-                quant_x(SLATE)
-            stage_b(c)
-            scatter(c - 1, 1)
+        group_w(3)
+        scatter(0, 0)
+        xc[1] = reuse.tile([P, GATHERS[1][1]], U32, name="y00", align_bytes=64)
+        quant_x(1)
+        stage_b(1)
+        scatter(0, 1)
+        group_w(4)
+        scatter(1, 0)
+        stage_b(2)
+        xc[2] = reuse.tile([P, GATHERS[2][1]], U32, name="wg2", align_bytes=64)
+        quant_x(2)
+        scatter(1, 1)
+        scatter(2, 0)
+        gather_planes(SLATE, xplane)
+        weave_x(SLATE)
+        stage_b(3)
+        scatter(2, 1)
+        scatter(3, 0)
+        quant_x(SLATE)
+        stage_b(4)
+        scatter(3, 1)
         scatter(NCH - 1, 0)
         nc.sync.dma_start(out[0:P, :], win[0][:])
         scatter(NCH - 1, 1)

@@ -13,7 +13,6 @@ U8 = mybir.dt.uint8
 FP8X4 = mybir.dt.float8_e4m3fn_x4
 MULT = mybir.AluOpType.mult
 ADD = mybir.AluOpType.add
-COPY = mybir.ActivationFunctionType.Copy
 
 P = 128
 HALF = T // 2
@@ -21,18 +20,16 @@ GRP = 4
 GATHERS = ((0, 512), (512, 512), (1024, 512), (1536, 512))
 CHUNKS = ((0, 256), (256, 256), (512, 512), (1024, 512), (1536, 512))
 CAST_SPLIT = ((("v", 0, 512), ("s", 512, 768), ("g", 768, 1024)), (("s", 0, 512), ("g", 512, 1024)))
-IENG = "gggg"
-DENG = "sssssssg"
-WG_BUFS = 2
-SLATE = 3
+CODES_AFTER = {1: 0, 2: 2, 3: 3}
+OWN_WG = (0, 2, 3)
 
 
 def tile_routed_moe_kernel(tc, xT, w, offs, out):
     nc = tc.nc
     with ExitStack() as ctx:
         held = ctx.enter_context(tc.tile_pool(name="held", bufs=1))
-        wraw_pool = ctx.enter_context(tc.tile_pool(name="wraw", bufs=6))
-        wgrp_pool = ctx.enter_context(tc.tile_pool(name="wgrp", bufs=WG_BUFS))
+        wraw_pool = ctx.enter_context(tc.tile_pool(name="wraw", bufs=3))
+        wgrp_pool = ctx.enter_context(tc.tile_pool(name="wgrp", bufs=2))
         y_pool = ctx.enter_context(tc.tile_pool(name="ypool", bufs=4))
         reuse = ctx.enter_context(tc.tile_pool(name="reuse", bufs=1))
         psum = ctx.enter_context(tc.psum_pool(name="psum", bufs=1))
@@ -49,7 +46,10 @@ def tile_routed_moe_kernel(tc, xT, w, offs, out):
                 xraw[(u, h)] = xr
         wraw = []
         for i in range(E // 2):
-            wr = wraw_pool.tile([P, 2, 4, N], F32, name="wr")
+            if i % 2 == 1:
+                wr = reuse.tile([P, 2, 4, N], F32, name="wr%d" % i, align_bytes=64)
+            else:
+                wr = wraw_pool.tile([P, 2, 4, N], F32, name="wr")
             nc.sync.dma_start(wr[:], w[2 * i : 2 * i + 2].rearrange("e (p j) n -> p e j n", j=4))
             wraw.append(wr)
 
@@ -78,8 +78,8 @@ def tile_routed_moe_kernel(tc, xT, w, offs, out):
 
         NCH = len(CHUNKS)
         xg = [held.tile([P, 4 * n], BF16, name="xg%d" % i, align_bytes=64) for i, (s0, n) in enumerate(GATHERS)]
-        xw = [(reuse if i >= SLATE - 1 else held).tile([P, 4 * n], BF16, name="xw%d" % i, align_bytes=64) for i, (s0, n) in enumerate(GATHERS)]
-        xc = {i: held.tile([P, GATHERS[i][1]], U32, name="xc%d" % i, align_bytes=64) for i in (0, 3)}
+        xw = [held.tile([P, 4 * n], BF16, name="xw%d" % i, align_bytes=64) for i, (s0, n) in enumerate(GATHERS)]
+        xc = {0: held.tile([P, GATHERS[0][1]], U32, name="xc0", align_bytes=64)}
         xs = [held.tile([P, n], U8, name="xs%d" % i, align_bytes=64) for i, (s0, n) in enumerate(GATHERS)]
         wc = [held.tile([P, n // C * N], U32, name="wc%d" % c, align_bytes=64) for c, (s0, n) in enumerate(CHUNKS)]
         ws = [held.tile([P, n // C * N], U8, name="ws%d" % c, align_bytes=64) for c, (s0, n) in enumerate(CHUNKS)]
@@ -96,12 +96,6 @@ def tile_routed_moe_kernel(tc, xT, w, offs, out):
             dst = xw[i][:].bitcast(U32)[:, u * n : (u + 1) * n]
             nc.vector.tensor_copy(dst, xpair[u][:].bitcast(U32).indirect(offs_of(s0, n)))
 
-        def gather_planes(i, xplane):
-            s0, n = GATHERS[i]
-            for e in range(2):
-                dst = xw[i][:].rearrange("p (u n e) -> p u n e", u=2, e=2)[:, 1, :, e]
-                nc.scalar.activation(dst, xplane[:, e, :].indirect(offs_of(s0, n)), COPY)
-
         def weave_x(i):
             nc.gpsimd.tensor_copy(
                 xg[i][:].bitcast(U32).rearrange("p (n u) -> p n u", u=2),
@@ -109,6 +103,8 @@ def tile_routed_moe_kernel(tc, xT, w, offs, out):
             )
 
         def quant_x(i):
+            if i in CODES_AFTER:
+                xc[i] = reuse.tile([P, GATHERS[i][1]], U32, name="wg%d" % CODES_AFTER[i], align_bytes=64)
             nc.vector.quantize_mx(out=xc[i][:].bitcast(FP8X4), scales=xs[i][:], in_=xg[i][:])
 
         def piece_of(slot):
@@ -120,21 +116,18 @@ def tile_routed_moe_kernel(tc, xT, w, offs, out):
         def group_w(c):
             s0, n = CHUNKS[c]
             e0, ne = s0 // C, n // C
-            if c == 2:
-                wg = reuse.tile([P, ne * 4 * N], BF16, name="wg2", align_bytes=64)
+            if c in OWN_WG:
+                wg = reuse.tile([P, ne * 4 * N], BF16, name="wg%d" % c, align_bytes=64)
             else:
                 wg = wgrp_pool.tile([P, ne * 4 * N], BF16, name="wg", align_bytes=64)
             wgs[c] = wg
             for i in range(e0 // 2, (e0 + ne) // 2):
                 dst = wg[:, (2 * i - e0) * 4 * N : (2 * i - e0 + 2) * 4 * N]
-                if DENG[i] == "g":
-                    copy_on("g", dst.rearrange("p (e n j) -> p e n j", e=2, j=4), wraw[i][:].rearrange("p e j n -> p e n j"))
-                else:
-                    copy_on(
-                        DENG[i],
-                        dst.rearrange("p (e c i j) -> p e c j i", e=2, i=4, j=4),
-                        wraw[i][:].rearrange("p e j (c i) -> p e c j i", i=4),
-                    )
+                copy_on(
+                    "s",
+                    dst.rearrange("p (e c i j) -> p e c j i", e=2, i=4, j=4),
+                    wraw[i][:].rearrange("p e j (c i) -> p e c j i", i=4),
+                )
 
         def stage_b(c):
             s0, n = CHUNKS[c]
@@ -154,10 +147,9 @@ def tile_routed_moe_kernel(tc, xT, w, offs, out):
                         start=True,
                         stop=True,
                     )
-                if c == SLATE and mb == 1:
-                    y = reuse.tile([P, n], F32, name="xw%d" % SLATE, align_bytes=64)
-                elif c == 0 and mb == 0:
-                    y = reuse.tile([P, n], F32, name="y00", align_bytes=64)
+                if mb == 1 and c + 1 < NCH:
+                    s1, n1 = CHUNKS[c + 1]
+                    y = reuse.tile([P, n], F32, name="wr%d" % ((s1 + n1) // (2 * C) - 1), align_bytes=64)
                 else:
                     y = y_pool.tile([P, n], F32, name="y")
                 nc.scalar.copy(y[:], acc[mb][g][:, q0 * C : (q0 + ne) * C])
@@ -169,41 +161,34 @@ def tile_routed_moe_kernel(tc, xT, w, offs, out):
 
         for u in range(2):
             for i in range(len(GATHERS)):
-                if u == 0 or i != SLATE:
-                    gather(u, i)
+                gather(u, i)
         weave_x(0)
         quant_x(0)
         weave_x(1)
         weave_x(2)
-        xplane = reuse.tile([P, 2, T], BF16, name="xw%d" % (SLATE - 1), align_bytes=64)
-        copy_on("g", xplane[:, :, 0:HALF], xraw[(1, 0)][:])
-        copy_on("g", xplane[:, :, HALF:T], xraw[(1, 1)][:])
+        weave_x(3)
         group_w(0)
         group_w(1)
-        group_w(2)
         stage_b(0)
-        group_w(3)
-        scatter(0, 0)
-        xc[1] = reuse.tile([P, GATHERS[1][1]], U32, name="y00", align_bytes=64)
         quant_x(1)
+        group_w(2)
         stage_b(1)
+        scatter(0, 0)
         scatter(0, 1)
-        group_w(4)
-        scatter(1, 0)
+        group_w(3)
         stage_b(2)
-        xc[2] = reuse.tile([P, GATHERS[2][1]], U32, name="wg2", align_bytes=64)
         quant_x(2)
+        scatter(1, 0)
         scatter(1, 1)
-        scatter(2, 0)
-        gather_planes(SLATE, xplane)
-        weave_x(SLATE)
+        group_w(4)
         stage_b(3)
+        quant_x(3)
+        scatter(2, 0)
         scatter(2, 1)
-        scatter(3, 0)
-        quant_x(SLATE)
         stage_b(4)
+        scatter(3, 0)
         scatter(3, 1)
-        scatter(NCH - 1, 0)
+        scatter(4, 0)
         nc.sync.dma_start(out[0:P, :], win[0][:])
-        scatter(NCH - 1, 1)
+        scatter(4, 1)
         nc.sync.dma_start(out[P : 2 * P, :], win[1][:])

@@ -13,6 +13,7 @@ U8 = mybir.dt.uint8
 FP8X4 = mybir.dt.float8_e4m3fn_x4
 MULT = mybir.AluOpType.mult
 ADD = mybir.AluOpType.add
+COPY = mybir.ActivationFunctionType.Copy
 
 P = 128
 HALF = T // 2
@@ -20,8 +21,8 @@ GRP = 4
 GATHERS = ((0, 512), (512, 512), (1024, 512), (1536, 512))
 CHUNKS = ((0, 256), (256, 256), (512, 512), (1024, 512), (1536, 512))
 CAST_SPLIT = ((("v", 0, 512), ("s", 512, 768), ("g", 768, 1024)), (("s", 0, 512), ("g", 512, 1024)))
-CODES_AFTER = {1: 0, 2: 2, 3: 3}
-OWN_WG = (0, 2, 3)
+OWN_WG = (0, 2)
+SLATE = 3
 
 
 def tile_routed_moe_kernel(tc, xT, w, offs, out):
@@ -77,9 +78,9 @@ def tile_routed_moe_kernel(tc, xT, w, offs, out):
                         )
 
         NCH = len(CHUNKS)
-        xg = [held.tile([P, 4 * n], BF16, name="xg%d" % i, align_bytes=64) for i, (s0, n) in enumerate(GATHERS)]
-        xw = [held.tile([P, 4 * n], BF16, name="xw%d" % i, align_bytes=64) for i, (s0, n) in enumerate(GATHERS)]
-        xc = {0: held.tile([P, GATHERS[0][1]], U32, name="xc0", align_bytes=64)}
+        xg = [(reuse if i == 2 else held).tile([P, 4 * n], BF16, name="xg%d" % i, align_bytes=64) for i, (s0, n) in enumerate(GATHERS[:SLATE])]
+        xw = [(reuse if i == SLATE else held).tile([P, 4 * n], BF16, name="xw%d" % i, align_bytes=64) for i, (s0, n) in enumerate(GATHERS)]
+        xc = {0: held.tile([P, GATHERS[0][1]], U32, name="xc0", align_bytes=64)[:]}
         xs = [held.tile([P, n], U8, name="xs%d" % i, align_bytes=64) for i, (s0, n) in enumerate(GATHERS)]
         wc = [held.tile([P, n // C * N], U32, name="wc%d" % c, align_bytes=64) for c, (s0, n) in enumerate(CHUNKS)]
         ws = [held.tile([P, n // C * N], U8, name="ws%d" % c, align_bytes=64) for c, (s0, n) in enumerate(CHUNKS)]
@@ -96,6 +97,12 @@ def tile_routed_moe_kernel(tc, xT, w, offs, out):
             dst = xw[i][:].bitcast(U32)[:, u * n : (u + 1) * n]
             nc.vector.tensor_copy(dst, xpair[u][:].bitcast(U32).indirect(offs_of(s0, n)))
 
+        def gather_planes(i, xplane):
+            s0, n = GATHERS[i]
+            for e in range(2):
+                dst = xw[i][:].rearrange("p (u n e) -> p u n e", u=2, e=2)[:, 1, :, e]
+                nc.scalar.activation(dst, xplane[:, e * T : (e + 1) * T].indirect(offs_of(s0, n)), COPY)
+
         def weave_x(i):
             nc.gpsimd.tensor_copy(
                 xg[i][:].bitcast(U32).rearrange("p (n u) -> p n u", u=2),
@@ -103,9 +110,7 @@ def tile_routed_moe_kernel(tc, xT, w, offs, out):
             )
 
         def quant_x(i):
-            if i in CODES_AFTER:
-                xc[i] = reuse.tile([P, GATHERS[i][1]], U32, name="wg%d" % CODES_AFTER[i], align_bytes=64)
-            nc.vector.quantize_mx(out=xc[i][:].bitcast(FP8X4), scales=xs[i][:], in_=xg[i][:])
+            nc.vector.quantize_mx(out=xc[i].bitcast(FP8X4), scales=xs[i][:], in_=xg[i][:])
 
         def piece_of(slot):
             for i, (s0, n) in enumerate(GATHERS):
@@ -129,7 +134,7 @@ def tile_routed_moe_kernel(tc, xT, w, offs, out):
                     wraw[i][:].rearrange("p e j (c i) -> p e c j i", i=4),
                 )
 
-        def stage_b(c):
+        def stage_q(c):
             s0, n = CHUNKS[c]
             e0, ne = s0 // C, n // C
             g, q0 = e0 // GRP, e0 % GRP
@@ -147,13 +152,17 @@ def tile_routed_moe_kernel(tc, xT, w, offs, out):
                         start=True,
                         stop=True,
                     )
-                if mb == 1 and c + 1 < NCH:
-                    s1, n1 = CHUNKS[c + 1]
-                    y = reuse.tile([P, n], F32, name="wr%d" % ((s1 + n1) // (2 * C) - 1), align_bytes=64)
-                else:
-                    y = y_pool.tile([P, n], F32, name="y")
-                nc.scalar.copy(y[:], acc[mb][g][:, q0 * C : (q0 + ne) * C])
-                ys[(c, mb)] = y
+
+        def copy_y(c, mb, tag):
+            s0, n = CHUNKS[c]
+            e0, ne = s0 // C, n // C
+            g, q0 = e0 // GRP, e0 % GRP
+            if tag == "":
+                y = y_pool.tile([P, n], F32, name="y")
+            else:
+                y = reuse.tile([P, n], F32, name=tag, align_bytes=64)
+            nc.scalar.copy(y[:], acc[mb][g][:, q0 * C : (q0 + ne) * C])
+            ys[(c, mb)] = y
 
         def scatter(c, mb):
             s0, n = CHUNKS[c]
@@ -161,31 +170,50 @@ def tile_routed_moe_kernel(tc, xT, w, offs, out):
 
         for u in range(2):
             for i in range(len(GATHERS)):
-                gather(u, i)
+                if u == 0 or i != SLATE:
+                    gather(u, i)
         weave_x(0)
         quant_x(0)
         weave_x(1)
         weave_x(2)
-        weave_x(3)
         group_w(0)
         group_w(1)
-        stage_b(0)
+        stage_q(0)
+        copy_y(0, 0, "")
+        copy_y(0, 1, "wr1")
+        xc[1] = reuse.tile([P, GATHERS[1][1]], U32, name="wg0", align_bytes=64)[:]
         quant_x(1)
         group_w(2)
-        stage_b(1)
+        stage_q(1)
+        copy_y(1, 0, "")
+        copy_y(1, 1, "wr3")
         scatter(0, 0)
         scatter(0, 1)
         group_w(3)
-        stage_b(2)
+        stage_q(2)
+        copy_y(2, 0, "")
+        copy_y(2, 1, "wr5")
+        xc[2] = reuse.tile([P, GATHERS[2][1]], U32, name="wg2", align_bytes=64)[:]
         quant_x(2)
+        xplane = reuse.tile([P, 2 * T], BF16, name="xg2", align_bytes=64)[:]
+        copy_on("g", xplane.rearrange("p (e n) -> p e n", e=2)[:, :, 0:HALF], xraw[(1, 0)][:])
+        copy_on("g", xplane.rearrange("p (e n) -> p e n", e=2)[:, :, HALF:T], xraw[(1, 1)][:])
         scatter(1, 0)
         scatter(1, 1)
         group_w(4)
-        stage_b(3)
-        quant_x(3)
+        stage_q(3)
+        copy_y(3, 0, "")
+        gather_planes(SLATE, xplane)
+        xg.append(reuse.tile([P, 4 * GATHERS[SLATE][1]], BF16, name="wr7", align_bytes=64))
+        weave_x(SLATE)
+        copy_y(3, 1, "xw3")
         scatter(2, 0)
         scatter(2, 1)
-        stage_b(4)
+        xc[3] = reuse.tile([P, GATHERS[3][1]], U32, name="wr5", align_bytes=64)[:]
+        quant_x(3)
+        stage_q(4)
+        copy_y(4, 0, "")
+        copy_y(4, 1, "")
         scatter(3, 0)
         scatter(3, 1)
         scatter(4, 0)

@@ -16,11 +16,14 @@ ADD = mybir.AluOpType.add
 COPY = mybir.ActivationFunctionType.Copy
 
 P = 128
-HALF = T // 2
+XCUT = (1536, 1280)
 GRP = 4
 GATHERS = ((0, 512), (512, 512), (1024, 512), (1536, 512))
 CHUNKS = ((0, 256), (256, 256), (512, 512), (1024, 512), (1536, 512))
-CAST_SPLIT = ((("v", 0, 512), ("s", 512, 768), ("g", 768, 1024)), (("s", 0, 512), ("g", 512, 1024)))
+CAST_SPLIT = (
+    ((("v", 0, 784), ("s", 784, 1184), ("g", 1184, 1536)), (("v", 0, 288), ("s", 288, 416), ("g", 416, 512))),
+    ((("s", 0, 672), ("g", 672, 1280)), (("s", 0, 432), ("g", 432, 768))),
+)
 OWN_WG = (0, 2)
 SLATE = 3
 
@@ -42,8 +45,9 @@ def tile_routed_moe_kernel(tc, xT, w, offs, out):
         xraw = {}
         for u in range(2):
             for h in range(2):
-                xr = held.tile([P, 2, HALF], F32, name="xraw%d%d" % (u, h))
-                nc.sync.dma_start(xr[:], x_view[:, 2 * u : 2 * u + 2, h * HALF : (h + 1) * HALF])
+                t0, t1 = (0, XCUT[u], T)[h : h + 2]
+                xr = held.tile([P, 2, t1 - t0], F32, name="xraw%d%d" % (u, h))
+                nc.sync.dma_start(xr[:], x_view[:, 2 * u : 2 * u + 2, t0:t1])
                 xraw[(u, h)] = xr
         wraw = []
         for i in range(E // 2):
@@ -65,8 +69,8 @@ def tile_routed_moe_kernel(tc, xT, w, offs, out):
         xpair = [held.tile([P, 2 * T], BF16, name="xpair%d" % u) for u in range(2)]
         for u in range(2):
             for h in range(2):
-                for kind, n0, n1 in CAST_SPLIT[u]:
-                    dst = xpair[u][:, 2 * (h * HALF + n0) : 2 * (h * HALF + n1)]
+                for kind, n0, n1 in CAST_SPLIT[u][h]:
+                    dst = xpair[u][:, 2 * (h * XCUT[u] + n0) : 2 * (h * XCUT[u] + n1)]
                     src = xraw[(u, h)][:, :, n0:n1]
                     if kind == "g":
                         copy_on(kind, dst.rearrange("p (n e) -> p n e", e=2), src.rearrange("p e n -> p n e"))
@@ -196,8 +200,8 @@ def tile_routed_moe_kernel(tc, xT, w, offs, out):
         xc[2] = reuse.tile([P, GATHERS[2][1]], U32, name="wg2", align_bytes=64)[:]
         quant_x(2)
         xplane = reuse.tile([P, 2 * T], BF16, name="xg2", align_bytes=64)[:]
-        copy_on("g", xplane.rearrange("p (e n) -> p e n", e=2)[:, :, 0:HALF], xraw[(1, 0)][:])
-        copy_on("g", xplane.rearrange("p (e n) -> p e n", e=2)[:, :, HALF:T], xraw[(1, 1)][:])
+        copy_on("g", xplane.rearrange("p (e n) -> p e n", e=2)[:, :, 0 : XCUT[1]], xraw[(1, 0)][:])
+        copy_on("g", xplane.rearrange("p (e n) -> p e n", e=2)[:, :, XCUT[1] : T], xraw[(1, 1)][:])
         scatter(1, 0)
         scatter(1, 1)
         group_w(4)

@@ -21,7 +21,7 @@ GRP = 4
 GATHERS = ((0, 512), (512, 512), (1024, 512), (1536, 512))
 CHUNKS = ((0, 256), (256, 256), (512, 512), (1024, 512), (1536, 512))
 CAST_SPLIT = (
-    ((("v", 0, 784), ("s", 784, 1184), ("g", 1184, 1536)), (("v", 0, 288), ("s", 288, 416), ("g", 416, 512))),
+    ((("v", 0, 1008), ("s", 1008, 1536)), (("v", 0, 336), ("s", 336, 512))),
     ((("s", 0, 672), ("g", 672, 1280)), (("s", 0, 432), ("g", 432, 768))),
 )
 OWN_WG = (0, 2)

@@ -24,7 +24,7 @@ CAST_SPLIT = (
     ((("v", 0, 1008), ("s", 1008, 1536)), (("v", 0, 336), ("s", 336, 512))),
     ((("s", 0, 672), ("g", 672, 1280)), (("s", 0, 432), ("g", 432, 768))),
 )
-OWN_WG = (0, 2)
+OWN_WG = (0, 1, 2)
 SLATE = 3
 
 
@@ -82,8 +82,8 @@ def tile_routed_moe_kernel(tc, xT, w, offs, out):
                         )
 
         NCH = len(CHUNKS)
-        xg = [(reuse if i == 2 else held).tile([P, 4 * n], BF16, name="xg%d" % i, align_bytes=64) for i, (s0, n) in enumerate(GATHERS[:SLATE])]
-        xw = [(reuse if i == SLATE else held).tile([P, 4 * n], BF16, name="xw%d" % i, align_bytes=64) for i, (s0, n) in enumerate(GATHERS)]
+        xg = [held.tile([P, 4 * n], BF16, name="xg%d" % i, align_bytes=64) for i, (s0, n) in enumerate(GATHERS[:2])]
+        xw = [(reuse if i >= 2 else held).tile([P, 4 * n], BF16, name="xw%d" % i, align_bytes=64) for i, (s0, n) in enumerate(GATHERS)]
         xc = {0: held.tile([P, GATHERS[0][1]], U32, name="xc0", align_bytes=64)[:]}
         xs = [held.tile([P, n], U8, name="xs%d" % i, align_bytes=64) for i, (s0, n) in enumerate(GATHERS)]
         wc = [held.tile([P, n // C * N], U32, name="wc%d" % c, align_bytes=64) for c, (s0, n) in enumerate(CHUNKS)]
@@ -179,7 +179,6 @@ def tile_routed_moe_kernel(tc, xT, w, offs, out):
         weave_x(0)
         quant_x(0)
         weave_x(1)
-        weave_x(2)
         group_w(0)
         group_w(1)
         stage_q(0)
@@ -187,6 +186,8 @@ def tile_routed_moe_kernel(tc, xT, w, offs, out):
         copy_y(0, 1, "wr1")
         xc[1] = reuse.tile([P, GATHERS[1][1]], U32, name="wg0", align_bytes=64)[:]
         quant_x(1)
+        xg.append(reuse.tile([P, 4 * GATHERS[2][1]], BF16, name="wg1", align_bytes=64))
+        weave_x(2)
         group_w(2)
         stage_q(1)
         copy_y(1, 0, "")
@@ -199,7 +200,7 @@ def tile_routed_moe_kernel(tc, xT, w, offs, out):
         copy_y(2, 1, "wr5")
         xc[2] = reuse.tile([P, GATHERS[2][1]], U32, name="wg2", align_bytes=64)[:]
         quant_x(2)
-        xplane = reuse.tile([P, 2 * T], BF16, name="xg2", align_bytes=64)[:]
+        xplane = reuse.tile([P, 2 * T], BF16, name="wg1", align_bytes=64)[:]
         copy_on("g", xplane.rearrange("p (e n) -> p e n", e=2)[:, :, 0 : XCUT[1]], xraw[(1, 0)][:])
         copy_on("g", xplane.rearrange("p (e n) -> p e n", e=2)[:, :, XCUT[1] : T], xraw[(1, 1)][:])
         scatter(1, 0)

@@ -24,7 +24,6 @@ CAST_SPLIT = (
     ((("v", 0, 1008), ("s", 1008, 1536)), (("v", 0, 336), ("s", 336, 512))),
     ((("s", 0, 672), ("g", 672, 1280)), (("s", 0, 432), ("g", 432, 768))),
 )
-OWN_WG = (0, 1, 2)
 SLATE = 3
 
 
@@ -33,7 +32,6 @@ def tile_routed_moe_kernel(tc, xT, w, offs, out):
     with ExitStack() as ctx:
         held = ctx.enter_context(tc.tile_pool(name="held", bufs=1))
         wraw_pool = ctx.enter_context(tc.tile_pool(name="wraw", bufs=3))
-        wgrp_pool = ctx.enter_context(tc.tile_pool(name="wgrp", bufs=2))
         y_pool = ctx.enter_context(tc.tile_pool(name="ypool", bufs=4))
         reuse = ctx.enter_context(tc.tile_pool(name="reuse", bufs=1))
         psum = ctx.enter_context(tc.psum_pool(name="psum", bufs=1))
@@ -51,7 +49,7 @@ def tile_routed_moe_kernel(tc, xT, w, offs, out):
                 xraw[(u, h)] = xr
         wraw = []
         for i in range(E // 2):
-            if i % 2 == 1:
+            if i % 2 == 1 or i == 6:
                 wr = reuse.tile([P, 2, 4, N], F32, name="wr%d" % i, align_bytes=64)
             else:
                 wr = wraw_pool.tile([P, 2, 4, N], F32, name="wr")
@@ -83,7 +81,7 @@ def tile_routed_moe_kernel(tc, xT, w, offs, out):
 
         NCH = len(CHUNKS)
         xg = [held.tile([P, 4 * n], BF16, name="xg%d" % i, align_bytes=64) for i, (s0, n) in enumerate(GATHERS[:2])]
-        xw = [(reuse if i >= 2 else held).tile([P, 4 * n], BF16, name="xw%d" % i, align_bytes=64) for i, (s0, n) in enumerate(GATHERS)]
+        xw = [held.tile([P, (2 if i == SLATE else 4) * n], BF16, name="xw%d" % i, align_bytes=64) for i, (s0, n) in enumerate(GATHERS)]
         xc = {0: held.tile([P, GATHERS[0][1]], U32, name="xc0", align_bytes=64)[:]}
         xs = [held.tile([P, n], U8, name="xs%d" % i, align_bytes=64) for i, (s0, n) in enumerate(GATHERS)]
         wc = [held.tile([P, n // C * N], U32, name="wc%d" % c, align_bytes=64) for c, (s0, n) in enumerate(CHUNKS)]
@@ -101,17 +99,28 @@ def tile_routed_moe_kernel(tc, xT, w, offs, out):
             dst = xw[i][:].bitcast(U32)[:, u * n : (u + 1) * n]
             nc.vector.tensor_copy(dst, xpair[u][:].bitcast(U32).indirect(offs_of(s0, n)))
 
-        def gather_planes(i, xplane):
+        xplane = []
+
+        def cast_plane(e, tag):
+            xp = reuse.tile([P, T], BF16, name=tag, align_bytes=64)
+            for h in range(2):
+                t0, t1 = (0, XCUT[1], T)[h : h + 2]
+                copy_on("g", xp[:, t0:t1], xraw[(1, h)][:, e])
+            xplane.append(xp)
+
+        def gather_planes(i, run):
             s0, n = GATHERS[i]
             for e in range(2):
-                dst = xw[i][:].rearrange("p (u n e) -> p u n e", u=2, e=2)[:, 1, :, e]
-                nc.scalar.activation(dst, xplane[:, e * T : (e + 1) * T].indirect(offs_of(s0, n)), COPY)
+                nc.scalar.activation(run.rearrange("p (n e) -> p n e", e=2)[:, :, e], xplane[e][:].indirect(offs_of(s0, n)), COPY)
 
         def weave_x(i):
             nc.gpsimd.tensor_copy(
                 xg[i][:].bitcast(U32).rearrange("p (n u) -> p n u", u=2),
                 xw[i][:].bitcast(U32).rearrange("p (u n) -> p n u", u=2),
             )
+
+        def weave_half(i, u, run):
+            nc.gpsimd.tensor_copy(xg[i][:].bitcast(U32).rearrange("p (n u) -> p u n", u=2)[:, u], run.bitcast(U32))
 
         def quant_x(i):
             nc.vector.quantize_mx(out=xc[i].bitcast(FP8X4), scales=xs[i][:], in_=xg[i][:])
@@ -122,16 +131,11 @@ def tile_routed_moe_kernel(tc, xT, w, offs, out):
                     return i, slot - s0
             raise ValueError("slot")
 
-        def group_w(c):
-            s0, n = CHUNKS[c]
-            e0, ne = s0 // C, n // C
-            if c in OWN_WG:
-                wg = reuse.tile([P, ne * 4 * N], BF16, name="wg%d" % c, align_bytes=64)
-            else:
-                wg = wgrp_pool.tile([P, ne * 4 * N], BF16, name="wg", align_bytes=64)
-            wgs[c] = wg
-            for i in range(e0 // 2, (e0 + ne) // 2):
-                dst = wg[:, (2 * i - e0) * 4 * N : (2 * i - e0 + 2) * 4 * N]
+        def group_w(c, i0, i1, tag):
+            wg = reuse.tile([P, (i1 - i0) * 8 * N], BF16, name=tag, align_bytes=64)
+            wgs.setdefault(c, []).append((wg, (i1 - i0) * 2 * N))
+            for i in range(i0, i1):
+                dst = wg[:, (i - i0) * 8 * N : (i - i0 + 1) * 8 * N]
                 copy_on(
                     "s",
                     dst.rearrange("p (e c i j) -> p e c j i", e=2, i=4, j=4),
@@ -142,7 +146,11 @@ def tile_routed_moe_kernel(tc, xT, w, offs, out):
             s0, n = CHUNKS[c]
             e0, ne = s0 // C, n // C
             g, q0 = e0 // GRP, e0 % GRP
-            nc.vector.quantize_mx(out=wc[c][:].bitcast(FP8X4), scales=ws[c][:], in_=wgs[c][:])
+            w0 = 0
+            for wg, count in wgs[c]:
+                w1 = w0 + count
+                nc.vector.quantize_mx(out=wc[c][:, w0:w1].bitcast(FP8X4), scales=ws[c][:, w0:w1], in_=wg[:])
+                w0 = w1
             for mb in range(2):
                 for q in range(ne):
                     wcols = slice(q * N + mb * P, q * N + (mb + 1) * P)
@@ -166,11 +174,11 @@ def tile_routed_moe_kernel(tc, xT, w, offs, out):
             else:
                 y = reuse.tile([P, n], F32, name=tag, align_bytes=64)
             nc.scalar.copy(y[:], acc[mb][g][:, q0 * C : (q0 + ne) * C])
-            ys[(c, mb)] = y
+            ys[(c, mb)] = y[:]
 
         def scatter(c, mb):
             s0, n = CHUNKS[c]
-            nc.vector.tensor_copy(win[mb][:].indirect(offs_of(s0, n)), ys[(c, mb)][:])
+            nc.vector.tensor_copy(win[mb][:].indirect(offs_of(s0, n)), ys[(c, mb)])
 
         for u in range(2):
             for i in range(len(GATHERS)):
@@ -179,42 +187,44 @@ def tile_routed_moe_kernel(tc, xT, w, offs, out):
         weave_x(0)
         quant_x(0)
         weave_x(1)
-        group_w(0)
-        group_w(1)
+        group_w(0, 0, 1, "wg0")
+        group_w(1, 1, 2, "wg1")
         stage_q(0)
         copy_y(0, 0, "")
         copy_y(0, 1, "wr1")
         xc[1] = reuse.tile([P, GATHERS[1][1]], U32, name="wg0", align_bytes=64)[:]
         quant_x(1)
-        xg.append(reuse.tile([P, 4 * GATHERS[2][1]], BF16, name="wg1", align_bytes=64))
-        weave_x(2)
-        group_w(2)
+        group_w(2, 2, 4, "wg2")
         stage_q(1)
+        cast_plane(0, "wg1")
         copy_y(1, 0, "")
         copy_y(1, 1, "wr3")
         scatter(0, 0)
         scatter(0, 1)
-        group_w(3)
+        group_w(3, 4, 6, "wg3")
         stage_q(2)
         copy_y(2, 0, "")
         copy_y(2, 1, "wr5")
-        xc[2] = reuse.tile([P, GATHERS[2][1]], U32, name="wg2", align_bytes=64)[:]
+        xg.append(reuse.tile([P, 4 * GATHERS[2][1]], BF16, name="wg2", align_bytes=64))
+        weave_x(2)
+        xc[2] = held.tile([P, GATHERS[2][1]], U32, name="xc2", align_bytes=64)[:]
         quant_x(2)
-        xplane = reuse.tile([P, 2 * T], BF16, name="wg1", align_bytes=64)[:]
-        copy_on("g", xplane.rearrange("p (e n) -> p e n", e=2)[:, :, 0 : XCUT[1]], xraw[(1, 0)][:])
-        copy_on("g", xplane.rearrange("p (e n) -> p e n", e=2)[:, :, XCUT[1] : T], xraw[(1, 1)][:])
+        cast_plane(1, "wg2")
         scatter(1, 0)
         scatter(1, 1)
-        group_w(4)
+        group_w(4, 6, 7, "wg4")
         stage_q(3)
         copy_y(3, 0, "")
-        gather_planes(SLATE, xplane)
-        xg.append(reuse.tile([P, 4 * GATHERS[SLATE][1]], BF16, name="wr7", align_bytes=64))
-        weave_x(SLATE)
-        copy_y(3, 1, "xw3")
+        run3 = reuse.tile([P, 2 * GATHERS[SLATE][1]], BF16, name="wr6", align_bytes=64)
+        gather_planes(SLATE, run3[:])
+        group_w(4, 7, 8, "wg1")
+        xg.append(reuse.tile([P, 4 * GATHERS[SLATE][1]], BF16, name="wg3", align_bytes=64))
+        weave_half(SLATE, 0, xw[SLATE][:])
+        weave_half(SLATE, 1, run3[:])
+        copy_y(3, 1, "wr7")
         scatter(2, 0)
         scatter(2, 1)
-        xc[3] = reuse.tile([P, GATHERS[3][1]], U32, name="wr5", align_bytes=64)[:]
+        xc[3] = held.tile([P, GATHERS[3][1]], U32, name="xc3", align_bytes=64)[:]
         quant_x(3)
         stage_q(4)
         copy_y(4, 0, "")

@@ -37,8 +37,6 @@ def tile_routed_moe_kernel(tc, xT, w, offs, out):
         psum = ctx.enter_context(tc.psum_pool(name="psum", bufs=1))
 
         offsets = held.tile([P, E * C // 16], U16, name="offsets")
-        nc.sync.dma_start(offsets[:], offs)
-
         x_view = xT.rearrange("(p t) n -> p t n", t=4)
         xraw = {}
         for u in range(2):
@@ -47,6 +45,8 @@ def tile_routed_moe_kernel(tc, xT, w, offs, out):
                 xr = held.tile([P, 2, t1 - t0], F32, name="xraw%d%d" % (u, h))
                 nc.sync.dma_start(xr[:], x_view[:, 2 * u : 2 * u + 2, t0:t1])
                 xraw[(u, h)] = xr
+                if (u, h) == (0, 0):
+                    nc.sync.dma_start(offsets[:], offs)
         wraw = []
         for i in range(E // 2):
             if i % 2 == 1 or i == 6:
@@ -81,7 +81,7 @@ def tile_routed_moe_kernel(tc, xT, w, offs, out):
 
         NCH = len(CHUNKS)
         xg = [held.tile([P, 4 * n], BF16, name="xg%d" % i, align_bytes=64) for i, (s0, n) in enumerate(GATHERS[:2])]
-        xw = [held.tile([P, (2 if i == SLATE else 4) * n], BF16, name="xw%d" % i, align_bytes=64) for i, (s0, n) in enumerate(GATHERS)]
+        runs = held.tile([P, 2, T], U32, name="runs", align_bytes=64)
         xc = {0: held.tile([P, GATHERS[0][1]], U32, name="xc0", align_bytes=64)[:]}
         xs = [held.tile([P, n], U8, name="xs%d" % i, align_bytes=64) for i, (s0, n) in enumerate(GATHERS)]
         wc = [held.tile([P, n // C * N], U32, name="wc%d" % c, align_bytes=64) for c, (s0, n) in enumerate(CHUNKS)]
@@ -94,10 +94,12 @@ def tile_routed_moe_kernel(tc, xT, w, offs, out):
         def offs_of(s0, n):
             return offsets[:, s0 // 16 : (s0 + n) // 16]
 
-        def gather(u, i):
+        def gather(u, s0, n):
+            nc.vector.tensor_copy(runs[:, u, s0 : s0 + n], xpair[u][:].bitcast(U32).indirect(offs_of(s0, n)))
+
+        def run(i, u):
             s0, n = GATHERS[i]
-            dst = xw[i][:].bitcast(U32)[:, u * n : (u + 1) * n]
-            nc.vector.tensor_copy(dst, xpair[u][:].bitcast(U32).indirect(offs_of(s0, n)))
+            return runs[:, u, s0 : s0 + n]
 
         xplane = []
 
@@ -114,13 +116,14 @@ def tile_routed_moe_kernel(tc, xT, w, offs, out):
                 nc.scalar.activation(run.rearrange("p (n e) -> p n e", e=2)[:, :, e], xplane[e][:].indirect(offs_of(s0, n)), COPY)
 
         def weave_x(i):
+            s0, n = GATHERS[i]
             nc.gpsimd.tensor_copy(
                 xg[i][:].bitcast(U32).rearrange("p (n u) -> p n u", u=2),
-                xw[i][:].bitcast(U32).rearrange("p (u n) -> p n u", u=2),
+                runs[:, :, s0 : s0 + n].rearrange("p u n -> p n u"),
             )
 
-        def weave_half(i, u, run):
-            nc.gpsimd.tensor_copy(xg[i][:].bitcast(U32).rearrange("p (n u) -> p u n", u=2)[:, u], run.bitcast(U32))
+        def weave_half(i, u, words):
+            nc.gpsimd.tensor_copy(xg[i][:].bitcast(U32).rearrange("p (n u) -> p u n", u=2)[:, u], words)
 
         def quant_x(i):
             nc.vector.quantize_mx(out=xc[i].bitcast(FP8X4), scales=xs[i][:], in_=xg[i][:])
@@ -180,10 +183,10 @@ def tile_routed_moe_kernel(tc, xT, w, offs, out):
             s0, n = CHUNKS[c]
             nc.vector.tensor_copy(win[mb][:].indirect(offs_of(s0, n)), ys[(c, mb)])
 
-        for u in range(2):
-            for i in range(len(GATHERS)):
-                if u == 0 or i != SLATE:
-                    gather(u, i)
+        for s0 in range(0, T, 1024):
+            gather(0, s0, 1024)
+        for i in range(SLATE):
+            gather(1, *GATHERS[i])
         weave_x(0)
         quant_x(0)
         weave_x(1)
@@ -219,8 +222,8 @@ def tile_routed_moe_kernel(tc, xT, w, offs, out):
         gather_planes(SLATE, run3[:])
         group_w(4, 7, 8, "wg1")
         xg.append(reuse.tile([P, 4 * GATHERS[SLATE][1]], BF16, name="wg3", align_bytes=64))
-        weave_half(SLATE, 0, xw[SLATE][:])
-        weave_half(SLATE, 1, run3[:])
+        weave_half(SLATE, 0, run(SLATE, 0))
+        weave_half(SLATE, 1, run3[:].bitcast(U32))
         copy_y(3, 1, "wr7")
         scatter(2, 0)
         scatter(2, 1)

@@ -24,6 +24,8 @@ CAST_SPLIT = (
     ((("v", 0, 1008), ("s", 1008, 1536)), (("v", 0, 336), ("s", 336, 512))),
     ((("s", 0, 672), ("g", 672, 1280)), (("s", 0, 432), ("g", 432, 768))),
 )
+LOADS = ((0, 1), (1, 1), (2, 1), (3, 1), (4, 1), (6, 2), (5, 1), (8, 2), (10, 2), (12, 2), (14, 2))
+LENT = (4, 5, 10, 12, 14)
 SLATE = 3
 
 
@@ -31,7 +33,6 @@ def tile_routed_moe_kernel(tc, xT, w, offs, out):
     nc = tc.nc
     with ExitStack() as ctx:
         held = ctx.enter_context(tc.tile_pool(name="held", bufs=1))
-        wraw_pool = ctx.enter_context(tc.tile_pool(name="wraw", bufs=3))
         y_pool = ctx.enter_context(tc.tile_pool(name="ypool", bufs=4))
         reuse = ctx.enter_context(tc.tile_pool(name="reuse", bufs=1))
         psum = ctx.enter_context(tc.psum_pool(name="psum", bufs=1))
@@ -48,13 +49,10 @@ def tile_routed_moe_kernel(tc, xT, w, offs, out):
                 if (u, h) == (0, 0):
                     nc.sync.dma_start(offsets[:], offs)
         wraw = []
-        for i in range(E // 2):
-            if i % 2 == 1 or i == 6:
-                wr = reuse.tile([P, 2, 4, N], F32, name="wr%d" % i, align_bytes=64)
-            else:
-                wr = wraw_pool.tile([P, 2, 4, N], F32, name="wr")
-            nc.sync.dma_start(wr[:], w[2 * i : 2 * i + 2].rearrange("e (p j) n -> p e j n", j=4))
-            wraw.append(wr)
+        for e, count in LOADS:
+            wr = (reuse if e in LENT else held).tile([P, count, 4, N], F32, name="we%d" % e, align_bytes=64)
+            nc.sync.dma_start(wr[:], w[e : e + count].rearrange("e (p j) n -> p e j n", j=4))
+            wraw.append((e, count, wr))
 
         def copy_on(kind, dst, src):
             if kind == "v":
@@ -137,13 +135,14 @@ def tile_routed_moe_kernel(tc, xT, w, offs, out):
         def group_w(c, i0, i1, tag):
             wg = reuse.tile([P, (i1 - i0) * 8 * N], BF16, name=tag, align_bytes=64)
             wgs.setdefault(c, []).append((wg, (i1 - i0) * 2 * N))
-            for i in range(i0, i1):
-                dst = wg[:, (i - i0) * 8 * N : (i - i0 + 1) * 8 * N]
-                copy_on(
-                    "s",
-                    dst.rearrange("p (e c i j) -> p e c j i", e=2, i=4, j=4),
-                    wraw[i][:].rearrange("p e j (c i) -> p e c j i", i=4),
-                )
+            for e, count, wr in wraw:
+                if 2 * i0 <= e < 2 * i1:
+                    dst = wg[:, (e - 2 * i0) * 4 * N : (e - 2 * i0 + count) * 4 * N]
+                    copy_on(
+                        "s",
+                        dst.rearrange("p (e c i j) -> p e c j i", e=count, i=4, j=4),
+                        wr[:].rearrange("p e j (c i) -> p e c j i", i=4),
+                    )
 
         def stage_q(c):
             s0, n = CHUNKS[c]
@@ -176,8 +175,13 @@ def tile_routed_moe_kernel(tc, xT, w, offs, out):
                 y = y_pool.tile([P, n], F32, name="y")
             else:
                 y = reuse.tile([P, n], F32, name=tag, align_bytes=64)
-            nc.scalar.copy(y[:], acc[mb][g][:, q0 * C : (q0 + ne) * C])
-            ys[(c, mb)] = y[:]
+            copy_y_to(c, mb, y[:])
+
+        def copy_y_to(c, mb, y):
+            s0, n = CHUNKS[c]
+            g, q0 = s0 // C // GRP, s0 // C % GRP
+            nc.scalar.copy(y, acc[mb][g][:, q0 * C : q0 * C + n])
+            ys[(c, mb)] = y
 
         def scatter(c, mb):
             s0, n = CHUNKS[c]
@@ -193,21 +197,22 @@ def tile_routed_moe_kernel(tc, xT, w, offs, out):
         group_w(0, 0, 1, "wg0")
         group_w(1, 1, 2, "wg1")
         stage_q(0)
-        copy_y(0, 0, "")
-        copy_y(0, 1, "wr1")
         xc[1] = reuse.tile([P, GATHERS[1][1]], U32, name="wg0", align_bytes=64)[:]
         quant_x(1)
         group_w(2, 2, 4, "wg2")
+        early = reuse.tile([P, 3, CHUNKS[0][1]], F32, name="we4", align_bytes=64)
+        copy_y_to(0, 0, early[:, 0])
+        copy_y_to(0, 1, early[:, 1])
         stage_q(1)
         cast_plane(0, "wg1")
-        copy_y(1, 0, "")
-        copy_y(1, 1, "wr3")
+        copy_y_to(1, 0, early[:, 2])
+        copy_y(1, 1, "we5")
         scatter(0, 0)
         scatter(0, 1)
         group_w(3, 4, 6, "wg3")
         stage_q(2)
         copy_y(2, 0, "")
-        copy_y(2, 1, "wr5")
+        copy_y(2, 1, "we10")
         xg.append(reuse.tile([P, 4 * GATHERS[2][1]], BF16, name="wg2", align_bytes=64))
         weave_x(2)
         xc[2] = held.tile([P, GATHERS[2][1]], U32, name="xc2", align_bytes=64)[:]
@@ -218,13 +223,13 @@ def tile_routed_moe_kernel(tc, xT, w, offs, out):
         group_w(4, 6, 7, "wg4")
         stage_q(3)
         copy_y(3, 0, "")
-        run3 = reuse.tile([P, 2 * GATHERS[SLATE][1]], BF16, name="wr6", align_bytes=64)
+        run3 = reuse.tile([P, 2 * GATHERS[SLATE][1]], BF16, name="we12", align_bytes=64)
         gather_planes(SLATE, run3[:])
         group_w(4, 7, 8, "wg1")
         xg.append(reuse.tile([P, 4 * GATHERS[SLATE][1]], BF16, name="wg3", align_bytes=64))
         weave_half(SLATE, 0, run(SLATE, 0))
         weave_half(SLATE, 1, run3[:].bitcast(U32))
-        copy_y(3, 1, "wr7")
+        copy_y(3, 1, "we14")
         scatter(2, 0)
         scatter(2, 1)
         xc[3] = held.tile([P, GATHERS[3][1]], U32, name="xc3", align_bytes=64)[:]

from contextlib import ExitStack

import concourse.mybir as mybir

K, T, E, C, N = 512, 2048, 16, 128, 256
FLOPS = 2 * K * N * E * C

F32 = mybir.dt.float32
BF16 = mybir.dt.bfloat16
U32 = mybir.dt.uint32
U16 = mybir.dt.uint16
U8 = mybir.dt.uint8
FP8X4 = mybir.dt.float8_e4m3fn_x4
MULT = mybir.AluOpType.mult
ADD = mybir.AluOpType.add
COPY = mybir.ActivationFunctionType.Copy

P = 128
XCUT = (1536, 1280)
GRP = 4
GATHERS = ((0, 512), (512, 512), (1024, 512), (1536, 512))
CHUNKS = ((0, 256), (256, 256), (512, 512), (1024, 512), (1536, 512))
CAST_SPLIT = (
    ((("v", 0, 1008), ("s", 1008, 1536)), (("v", 0, 336), ("s", 336, 512))),
    ((("s", 0, 672), ("g", 672, 1280)), (("s", 0, 432), ("g", 432, 768))),
)
LOADS = ((0, 1), (1, 1), (2, 1), (3, 1), (4, 1), (6, 2), (5, 1), (8, 2), (10, 2), (12, 2), (14, 2))
LENT = (4, 5, 10, 12, 14)
SLATE = 3


def tile_routed_moe_kernel(tc, xT, w, offs, out):
    nc = tc.nc
    with ExitStack() as ctx:
        held = ctx.enter_context(tc.tile_pool(name="held", bufs=1))
        y_pool = ctx.enter_context(tc.tile_pool(name="ypool", bufs=4))
        reuse = ctx.enter_context(tc.tile_pool(name="reuse", bufs=1))
        psum = ctx.enter_context(tc.psum_pool(name="psum", bufs=1))

        offsets = held.tile([P, E * C // 16], U16, name="offsets")
        x_view = xT.rearrange("(p t) n -> p t n", t=4)
        xraw = {}
        for u in range(2):
            for h in range(2):
                t0, t1 = (0, XCUT[u], T)[h : h + 2]
                xr = held.tile([P, 2, t1 - t0], F32, name="xraw%d%d" % (u, h))
                nc.sync.dma_start(xr[:], x_view[:, 2 * u : 2 * u + 2, t0:t1])
                xraw[(u, h)] = xr
                if (u, h) == (0, 0):
                    nc.sync.dma_start(offsets[:], offs)
        wraw = []
        for e, count in LOADS:
            wr = (reuse if e in LENT else held).tile([P, count, 4, N], F32, name="we%d" % e, align_bytes=64)
            nc.sync.dma_start(wr[:], w[e : e + count].rearrange("e (p j) n -> p e j n", j=4))
            wraw.append((e, count, wr))

        def copy_on(kind, dst, src):
            if kind == "v":
                nc.vector.tensor_copy(dst, src)
            elif kind == "s":
                nc.scalar.copy(dst, src)
            else:
                nc.gpsimd.tensor_scalar(dst, src, 1.0, 0.0, op0=MULT, op1=ADD)

        xpair = [held.tile([P, 2 * T], BF16, name="xpair%d" % u) for u in range(2)]
        for u in range(2):
            for h in range(2):
                for kind, n0, n1 in CAST_SPLIT[u][h]:
                    dst = xpair[u][:, 2 * (h * XCUT[u] + n0) : 2 * (h * XCUT[u] + n1)]
                    src = xraw[(u, h)][:, :, n0:n1]
                    if kind == "g":
                        copy_on(kind, dst.rearrange("p (n e) -> p n e", e=2), src.rearrange("p e n -> p n e"))
                    else:
                        copy_on(
                            kind,
                            dst.rearrange("p (c i e) -> p c e i", i=4, e=2),
                            src.rearrange("p e (c i) -> p c e i", i=4),
                        )

        NCH = len(CHUNKS)
        xg = [held.tile([P, 4 * n], BF16, name="xg%d" % i, align_bytes=64) for i, (s0, n) in enumerate(GATHERS[:2])]
        runs = held.tile([P, 2, T], U32, name="runs", align_bytes=64)
        xc = {0: held.tile([P, GATHERS[0][1]], U32, name="xc0", align_bytes=64)[:]}
        xs = [held.tile([P, n], U8, name="xs%d" % i, align_bytes=64) for i, (s0, n) in enumerate(GATHERS)]
        wc = [held.tile([P, n // C * N], U32, name="wc%d" % c, align_bytes=64) for c, (s0, n) in enumerate(CHUNKS)]
        ws = [held.tile([P, n // C * N], U8, name="ws%d" % c, align_bytes=64) for c, (s0, n) in enumerate(CHUNKS)]
        acc = [[psum.tile([P, GRP * C], F32, name="acc%d%d" % (mb, g)) for g in range(E // GRP)] for mb in range(2)]
        win = [held.tile([P, T], F32, name="win%d" % mb) for mb in range(2)]
        wgs = {}
        ys = {}

        def offs_of(s0, n):
            return offsets[:, s0 // 16 : (s0 + n) // 16]

        def gather(u, s0, n):
            nc.vector.tensor_copy(runs[:, u, s0 : s0 + n], xpair[u][:].bitcast(U32).indirect(offs_of(s0, n)))

        def run(i, u):
            s0, n = GATHERS[i]
            return runs[:, u, s0 : s0 + n]

        xplane = []

        def cast_plane(e, tag):
            xp = reuse.tile([P, T], BF16, name=tag, align_bytes=64)
            for h in range(2):
                t0, t1 = (0, XCUT[1], T)[h : h + 2]
                copy_on("g", xp[:, t0:t1], xraw[(1, h)][:, e])
            xplane.append(xp)

        def gather_planes(i, run):
            s0, n = GATHERS[i]
            for e in range(2):
                nc.scalar.activation(run.rearrange("p (n e) -> p n e", e=2)[:, :, e], xplane[e][:].indirect(offs_of(s0, n)), COPY)

        def weave_x(i):
            s0, n = GATHERS[i]
            nc.gpsimd.tensor_copy(
                xg[i][:].bitcast(U32).rearrange("p (n u) -> p n u", u=2),
                runs[:, :, s0 : s0 + n].rearrange("p u n -> p n u"),
            )

        def weave_half(i, u, words):
            nc.gpsimd.tensor_copy(xg[i][:].bitcast(U32).rearrange("p (n u) -> p u n", u=2)[:, u], words)

        def quant_x(i):
            nc.vector.quantize_mx(out=xc[i].bitcast(FP8X4), scales=xs[i][:], in_=xg[i][:])

        def piece_of(slot):
            for i, (s0, n) in enumerate(GATHERS):
                if s0 <= slot < s0 + n:
                    return i, slot - s0
            raise ValueError("slot")

        def group_w(c, i0, i1, tag):
            wg = reuse.tile([P, (i1 - i0) * 8 * N], BF16, name=tag, align_bytes=64)
            wgs.setdefault(c, []).append((wg, (i1 - i0) * 2 * N))
            for e, count, wr in wraw:
                if 2 * i0 <= e < 2 * i1:
                    dst = wg[:, (e - 2 * i0) * 4 * N : (e - 2 * i0 + count) * 4 * N]
                    copy_on(
                        "s",
                        dst.rearrange("p (e c i j) -> p e c j i", e=count, i=4, j=4),
                        wr[:].rearrange("p e j (c i) -> p e c j i", i=4),
                    )

        def stage_q(c):
            s0, n = CHUNKS[c]
            e0, ne = s0 // C, n // C
            g, q0 = e0 // GRP, e0 % GRP
            w0 = 0
            for wg, count in wgs[c]:
                w1 = w0 + count
                nc.vector.quantize_mx(out=wc[c][:, w0:w1].bitcast(FP8X4), scales=ws[c][:, w0:w1], in_=wg[:])
                w0 = w1
            for mb in range(2):
                for q in range(ne):
                    wcols = slice(q * N + mb * P, q * N + (mb + 1) * P)
                    i, r0 = piece_of(s0 + q * C)
                    nc.tensor.matmul_mx(
                        out=acc[mb][g][:, (q0 + q) * C : (q0 + q + 1) * C],
                        lhsT=wc[c][:, wcols].bitcast(FP8X4),
                        lhsT_scale=ws[c][:, wcols],
                        rhs=xc[i][:, r0 : r0 + C].bitcast(FP8X4),
                        rhs_scale=xs[i][:, r0 : r0 + C],
                        start=True,
                        stop=True,
                    )

        def copy_y(c, mb, tag):
            s0, n = CHUNKS[c]
            e0, ne = s0 // C, n // C
            g, q0 = e0 // GRP, e0 % GRP
            if tag == "":
                y = y_pool.tile([P, n], F32, name="y")
            else:
                y = reuse.tile([P, n], F32, name=tag, align_bytes=64)
            copy_y_to(c, mb, y[:])

        def copy_y_to(c, mb, y):
            s0, n = CHUNKS[c]
            g, q0 = s0 // C // GRP, s0 // C % GRP
            nc.scalar.copy(y, acc[mb][g][:, q0 * C : q0 * C + n])
            ys[(c, mb)] = y

        def scatter(c, mb):
            s0, n = CHUNKS[c]
            nc.vector.tensor_copy(win[mb][:].indirect(offs_of(s0, n)), ys[(c, mb)])

        for s0 in range(0, T, 1024):
            gather(0, s0, 1024)
        for i in range(SLATE):
            gather(1, *GATHERS[i])
        weave_x(0)
        quant_x(0)
        weave_x(1)
        group_w(0, 0, 1, "wg0")
        group_w(1, 1, 2, "wg1")
        stage_q(0)
        xc[1] = reuse.tile([P, GATHERS[1][1]], U32, name="wg0", align_bytes=64)[:]
        quant_x(1)
        group_w(2, 2, 4, "wg2")
        early = reuse.tile([P, 3, CHUNKS[0][1]], F32, name="we4", align_bytes=64)
        copy_y_to(0, 0, early[:, 0])
        copy_y_to(0, 1, early[:, 1])
        stage_q(1)
        cast_plane(0, "wg1")
        copy_y_to(1, 0, early[:, 2])
        copy_y(1, 1, "we5")
        scatter(0, 0)
        scatter(0, 1)
        group_w(3, 4, 6, "wg3")
        stage_q(2)
        copy_y(2, 0, "")
        copy_y(2, 1, "we10")
        xg.append(reuse.tile([P, 4 * GATHERS[2][1]], BF16, name="wg2", align_bytes=64))
        weave_x(2)
        xc[2] = held.tile([P, GATHERS[2][1]], U32, name="xc2", align_bytes=64)[:]
        quant_x(2)
        cast_plane(1, "wg2")
        scatter(1, 0)
        scatter(1, 1)
        group_w(4, 6, 7, "wg4")
        stage_q(3)
        copy_y(3, 0, "")
        run3 = reuse.tile([P, 2 * GATHERS[SLATE][1]], BF16, name="we12", align_bytes=64)
        gather_planes(SLATE, run3[:])
        group_w(4, 7, 8, "wg1")
        xg.append(reuse.tile([P, 4 * GATHERS[SLATE][1]], BF16, name="wg3", align_bytes=64))
        weave_half(SLATE, 0, run(SLATE, 0))
        weave_half(SLATE, 1, run3[:].bitcast(U32))
        copy_y(3, 1, "we14")
        scatter(2, 0)
        scatter(2, 1)
        xc[3] = held.tile([P, GATHERS[3][1]], U32, name="xc3", align_bytes=64)[:]
        quant_x(3)
        stage_q(4)
        copy_y(4, 0, "")
        copy_y(4, 1, "")
        scatter(3, 0)
        scatter(3, 1)
        scatter(4, 0)
        nc.sync.dma_start(out[0:P, :], win[0][:])
        scatter(4, 1)
        nc.sync.dma_start(out[P : 2 * P, :], win[1][:])
